import numpy as np
import ml_dtypes


def mxq(x, axis, fmt="e4m3"):
    dtype, down = {"e4m3": (ml_dtypes.float8_e4m3fn, 7), "e5m2": (ml_dtypes.float8_e5m2, 14)}[fmt]
    v = np.moveaxis(np.asarray(x, np.float32).astype(ml_dtypes.bfloat16).astype(np.float64), axis, -1)
    blocks = v.reshape(v.shape[:-1] + (-1, 32))
    amax = np.abs(blocks).max(-1, keepdims=True)
    byte = np.maximum(np.where(amax > 0, np.frexp(amax)[1] - 1 + 127, 0) - down, 1)
    scale = np.exp2(byte - 127.0)
    codes = (blocks / scale).astype(np.float32).astype(dtype).astype(np.float64)
    return np.moveaxis((codes * scale).reshape(v.shape), -1, axis)


WIDE = False


def mx_kscale(k):
    if not WIDE:
        return np.ones(k)
    levels = np.array([10, -10, 5, -5, 0])
    if k % 512:
        return np.exp2(np.random.permutation(np.resize(levels, k // 32))).repeat(32)
    a = np.empty((k // 512, 16))
    for p in range(k // 512):
        a[p, :8] = np.random.permutation(np.resize(levels, 8))
        for g in range(8):
            far = levels[np.abs(levels - a[p, g]) >= 10]
            a[p, g + 8] = far[np.random.randint(len(far))]
    return np.exp2(a.ravel()).repeat(32)


def f64(x):
    return np.asarray(x).astype(np.float64)


def striped(idx):
    return np.tile(np.asarray(idx).reshape(-1, 16).T, (8, 1)).astype(np.uint16)


def unstriped(offs):
    return offs[:16].T.reshape(-1).astype(np.int64)


E2M1 = np.array([0.0, 0.5, 1.0, 1.5, 2.0, 3.0, 4.0, 6.0, -0.0, -0.5, -1.0, -1.5, -2.0, -3.0, -4.0, -6.0])


def pack_weight(w, fmt):
    k, n = w.shape
    w = f64(np.asarray(w, np.float32).astype(ml_dtypes.bfloat16)).reshape(k // 32, 32, n)
    amax = np.abs(w).max(1)
    if fmt == "e4m3":
        byte = np.frexp(amax)[1] - 1 + 127 - 7
    else:
        mant, ex = np.frexp(amax / 6.0)
        byte = np.where(mant > 0.5, ex, ex - 1) + 127
    byte = np.clip(np.where(amax > 0, byte, 1), 1, 254)
    scaled = (w * np.exp2(127.0 - byte)[:, None, :]).reshape(k, n).astype(np.float32)
    by_word = np.ascontiguousarray(scaled.reshape(k // 512, 128, 4, n).transpose(0, 1, 3, 2))
    if fmt == "e4m3":
        words = by_word.astype(ml_dtypes.float8_e4m3fn).view(np.uint8)
    else:
        c = by_word.astype(ml_dtypes.float4_e2m1fn).view(np.uint8) & 0xF
        words = (c[..., 0::2] | (c[..., 1::2] << 4)).reshape(k // 512, 128, 2 * n)
    return np.ascontiguousarray(words), np.ascontiguousarray(byte.astype(np.uint8).reshape(k // 512, 16, n))


def unpack_weight(words, scales, fmt):
    g, _, n = scales.shape
    words = np.ascontiguousarray(words).reshape(g, 128, n, -1)
    if fmt == "e4m3":
        vals = words.view(ml_dtypes.float8_e4m3fn).astype(np.float64)
    else:
        nib = np.empty((g, 128, n, 4), np.uint8)
        nib[..., 0::2] = words & 0xF
        nib[..., 1::2] = words >> 4
        vals = E2M1[nib]
    vals = vals * np.repeat(np.exp2(scales.astype(np.float64) - 127.0), 8, axis=1)[..., None]
    return vals.transpose(0, 1, 3, 2).reshape(g * 512, n)


def softplus(v):
    return np.log(1.0 + np.exp(v))


def sigmoid(v):
    return 1.0 / (1.0 + np.exp(-v))


D, K, R, T, I, Q, U = 512, 512, 512, 2048, 512, 128, 1024


def setup_inputs():
    n = np.random.standard_normal
    idx2 = np.random.permutation(U)[:I]
    idx = np.random.permutation(T)[:I]
    fd = mx_kscale(D)
    fk = mx_kscale(K)
    fr = mx_kscale(R)
    keysp = pack_weight(n((D, T)) / fd[:, None], "e2m1")
    tabp = pack_weight(n((K, T)) / fk[:, None], "e2m1")
    return {
        "query": (n((D, Q)) * 0.9 / np.sqrt(D) * fd[:, None]).astype(np.float32),
        "keys_words": keysp[0],
        "keys_scales": keysp[1],
        "th": (np.random.uniform(-0.3, 0.6, (Q, 1))).astype(np.float32),
        "reserve": (np.random.uniform(50.0, 200.0, (Q, 1))).astype(np.float32),
        "tab_words": tabp[0],
        "tab_scales": tabp[1],
        "w1": (n((K, R)) * 1 / np.sqrt(K) * fk[:, None]).astype(np.float32),
        "gtab": (n((R, U))).astype(np.float32),
        "gout": (n((R, Q)) * 1 / np.sqrt(R) * fr[:, None]).astype(np.float32),
        "hsc": (np.random.uniform(0.7, 1.4, (R, 1)) / fr[:, None]).astype(np.float32),
        "old": (0.5 * n((Q, T))).astype(np.float32),
        "offs2": striped(idx2),
        "offs": striped(idx),
    }


def reference(query, keys_words, keys_scales, th, reserve, tab_words, tab_scales, w1, gtab, gout, hsc, old, offs2, offs):
    idx2 = unstriped(offs2)
    idx = unstriped(offs)
    keysu = unpack_weight(keys_words, keys_scales, "e2m1")
    tabu = unpack_weight(tab_words, tab_scales, "e2m1")
    queryq = mxq(f64(query), 0, "e4m3")
    keysidxg = keysu[:, idx]
    a = queryq.T @ keysidxg
    p = softplus(a - f64(th))
    z = np.sum(p, axis=1, keepdims=True) + f64(reserve)
    w1q = mxq(f64(w1), 0, "e4m3")
    tabidxg = tabu[:, idx]
    zh = w1q.T @ tabidxg
    hg = sigmoid(f64(gtab)[:, idx2])
    hv = zh * hg
    hs1 = hv * f64(hsc)
    goutq = mxq(f64(gout), 0, "e4m3")
    hs1q = mxq(hs1, 0, "e4m3")
    c0 = goutq.T @ hs1q
    dz = np.sum(c0 * p / np.square(z) * (-1.0), axis=1, keepdims=True)
    dp = c0 / z + dz
    da = dp * sigmoid(a - f64(th))
    gs = da * 512.0
    gf = np.zeros((Q, T))
    gf[:, idx] = gs
    y = f64(old) + gf
    return y

@@ -1,0 +1,188 @@
+from contextlib import ExitStack
+
+import concourse.mybir as mybir
+
+D, K, R, T, I, Q, U = 512, 512, 512, 2048, 512, 128, 1024
+FLOPS = 2 * D * Q * I + 2 * K * R * I + 2 * R * Q * I
+
+F32 = mybir.dt.float32
+BF16 = mybir.dt.bfloat16
+I32 = mybir.dt.int32
+U32 = mybir.dt.uint32
+U16 = mybir.dt.uint16
+U8 = mybir.dt.uint8
+FP8X4 = mybir.dt.float8_e4m3fn_x4
+FP4X4 = mybir.dt.float4_e2m1fn_x4
+ACT = mybir.ActivationFunctionType
+ALU = mybir.AluOpType
+
+P = 128
+PACK = 4
+GAIN = 512.0
+STORE_COLS = 512
+HALF = I // 2
+
+
+def tile_attend_blrgated_capped_kernel(tc, query, keys_words, keys_scales, th, reserve, tab_words, tab_scales,
+                                        w1, gtab, gout, hsc, old, offs2, offs, out):
+    nc = tc.nc
+    with ExitStack() as ctx:
+        sb = ctx.enter_context(tc.tile_pool(name="sb", bufs=1))
+        ps = ctx.enter_context(tc.psum_pool(name="ps", bufs=1))
+
+        def sbuf(name, shape, dtype, tag=None):
+            return sb.tile(shape, dtype, name=name, tag=tag or name, align_bytes=64)
+
+        idx = sbuf("idx", [P, I // 16], U16)
+        idx2 = sbuf("idx2", [P, I // 16], U16)
+        key_words = sbuf("key_words", [P, T], U16)
+        key_bytes = sbuf("key_bytes", [P, T], U8)
+        tab_wd = sbuf("tab_wd", [P, T], U16)
+        tab_bytes = sbuf("tab_bytes", [P, T], U8)
+        q_raw = sbuf("q_raw", [P, PACK, Q], F32)
+        g_raw = sbuf("g_raw", [P, PACK, Q], F32)
+        w_raw = sbuf("w_raw", [P, PACK, R], F32)
+        gate_pool = [sbuf("gate_pool%d" % t, [P, U], F32) for t in range(PACK)]
+        old_sb = sbuf("old_sb", [P, T], F32)
+        th_sb = sbuf("th_sb", [P, 1], F32)
+        res_sb = sbuf("res_sb", [P, 1], F32)
+        hsc_sb = sbuf("hsc_sb", [P, PACK], F32)
+        window = sbuf("window", [P, T], F32)
+        warm = sbuf("warm", [P, 1], F32)
+        warm_out = sbuf("warm_out", [P, 1], F32)
+
+        nc.vector.memset(key_bytes[:].bitcast(I32), 0)
+        nc.vector.memset(tab_bytes[:].bitcast(I32), 0)
+        nc.gpsimd.memset(warm[:], 0.0)
+        nc.scalar.activation(warm_out[:], warm[:], ACT.Sigmoid)
+
+        def load_scale_rows(dst, src):
+            for quad in range(4):
+                nc.sync.dma_start(dst[32 * quad: 32 * quad + 4, :].bitcast(I32),
+                                  src[0, 4 * quad: 4 * quad + 4, :].bitcast(I32))
+
+        gtab_rows = gtab.rearrange("(p t) u -> t p u", t=PACK)
+        nc.gpsimd.dma_start(th_sb[:], th)
+        nc.gpsimd.dma_start(hsc_sb[:], hsc.rearrange("(p t) o -> p (t o)", t=PACK))
+        nc.gpsimd.dma_start(res_sb[:], reserve)
+        nc.sync.dma_start(idx[:], offs)
+        nc.sync.dma_start(key_words[:].bitcast(I32), keys_words[0].bitcast(I32))
+        load_scale_rows(key_bytes, keys_scales)
+        nc.sync.dma_start(q_raw[:], query.rearrange("(p j) q -> p j q", j=PACK))
+        nc.sync.dma_start(tab_wd[:].bitcast(I32), tab_words[0].bitcast(I32))
+        nc.sync.dma_start(idx2[:], offs2)
+        nc.sync.dma_start(gate_pool[0][:], gtab_rows[0])
+        load_scale_rows(tab_bytes, tab_scales)
+        nc.sync.dma_start(w_raw[:], w1.rearrange("(p j) r -> p j r", j=PACK))
+        for t in range(1, PACK):
+            nc.sync.dma_start(gate_pool[t][:], gtab_rows[t])
+        nc.sync.dma_start(g_raw[:], gout.rearrange("(p j) q -> p j q", j=PACK))
+        nc.sync.dma_start(old_sb[:], old)
+
+        nc.vector.memset(window[:], 0.0)
+
+        neg_th = sbuf("neg_th", [P, 1], F32)
+        neg_th_s = sbuf("neg_th_s", [P, 1], F32)
+        res_s = sbuf("res_s", [P, 1], F32)
+        nc.gpsimd.tensor_scalar(neg_th[:], th_sb[:], -1.0, 0.0, ALU.mult, ALU.add)
+        nc.gpsimd.tensor_scalar(neg_th_s[:], th_sb[:], -1.0 / GAIN, 0.0, ALU.mult, ALU.add)
+        nc.gpsimd.tensor_scalar(res_s[:], res_sb[:], 1.0 / GAIN, 0.0, ALU.mult, ALU.add)
+
+        def quantise(name, grouped, cols):
+            codes = sbuf(name + "_codes", [P, cols], U32)
+            scales = sbuf(name + "_scales", [P, cols], U8)
+            nc.vector.quantize_mx(out=codes[:].bitcast(FP8X4), scales=scales[:], in_=grouped)
+            return codes, scales
+
+        def interleave(copy, name, raw, cols):
+            grouped = sbuf(name + "_grouped", [P, cols, PACK], BF16)
+            copy(grouped[:].rearrange("p (c i) t -> p c t i", i=4), raw.rearrange("p t (c i) -> p c t i", i=4))
+            return grouped[:].rearrange("p c t -> p (c t)")
+
+        def gather_packed(name, words, scale_bytes):
+            got_words = sbuf(name + "_got_words", [P, I], U16)
+            got_bytes = sbuf(name + "_got_bytes", [P, I], U8)
+            nc.vector.tensor_copy(got_words[:], words[:].indirect(idx[:]))
+            nc.vector.tensor_copy(got_bytes[:], scale_bytes[:].indirect(idx[:]))
+            return got_words, got_bytes
+
+        k_words, k_bytes = gather_packed("key", key_words, key_bytes)
+        q_codes, q_scales = quantise("q", interleave(nc.scalar.copy, "q", q_raw[:], Q), Q)
+        a_ps = ps.tile([P, I], F32, name="a_ps")
+        nc.tensor.matmul_mx(out=a_ps[:], lhsT=q_codes[:].bitcast(FP8X4), lhsT_scale=q_scales[:],
+                            rhs=k_words[:].bitcast(FP4X4), rhs_scale=k_bytes[:], start=True, stop=True)
+        sig = sbuf("sig", [P, I], F32)
+        relu_s = sbuf("relu_s", [P, I], F32)
+        relu_sum = sbuf("relu_sum", [P, 1], F32)
+        dist = sbuf("dist", [P, I], F32)
+        nc.scalar.activation(sig[:], a_ps[:], ACT.Sigmoid, bias=neg_th[:])
+        nc.scalar.activation(relu_s[:], a_ps[:], ACT.Relu, bias=neg_th_s[:], scale=1.0 / GAIN, accum_out=relu_sum[:])
+        nc.scalar.activation(dist[:], sig[:], ACT.Abs, bias=-0.5)
+        base = sbuf("base", [P, 1], F32)
+        nc.gpsimd.tensor_tensor(base[:], relu_sum[:], res_s[:], ALU.add)
+
+        t_words, t_bytes = gather_packed("tab", tab_wd, tab_bytes)
+        w_grouped = sbuf("w_grouped", [P, PACK, P, PACK], BF16)
+        nc.vector.tensor_copy(w_grouped[:].rearrange("p t m j -> p m j t"),
+                              w_raw[:].rearrange("p j (m t) -> p m j t", t=PACK))
+        w_codes, w_scales = quantise("w", w_grouped[:].rearrange("p t m j -> p (t m j)"), R)
+        halves = [slice(h * HALF, (h + 1) * HALF) for h in range(2)]
+        hs_rows = [sbuf("hs_rows%d" % h, [P, PACK, HALF], BF16) for h in range(2)]
+        zh_ps = [ps.tile([P, I], F32, name="zh_ps%d" % t) for t in range(PACK)]
+        gate = [sbuf("gate%d" % t, [P, I], F32) for t in range(PACK)]
+
+        def gated(t, h):
+            nc.vector.scalar_tensor_tensor(hs_rows[h][:, t, :], zh_ps[t][:, halves[h]], hsc_sb[:, t: t + 1],
+                                           gate[t][:, halves[h]], ALU.mult, ALU.mult)
+
+        for t in range(PACK):
+            cols = slice(t * P, (t + 1) * P)
+            nc.tensor.matmul_mx(out=zh_ps[t][:], lhsT=w_codes[:, cols].bitcast(FP8X4), lhsT_scale=w_scales[:, cols],
+                                rhs=t_words[:].bitcast(FP4X4), rhs_scale=t_bytes[:], start=True, stop=True)
+        for t in range(PACK - 1):
+            nc.scalar.activation(gate[t][:], gate_pool[t][:].indirect(idx2[:]), ACT.Sigmoid)
+            for h in range(2):
+                gated(t, h)
+        last = PACK - 1
+        for h in range(2):
+            nc.scalar.activation(gate[last][:, halves[h]],
+                                 gate_pool[last][:].indirect(idx2[:, h * HALF // 16: (h + 1) * HALF // 16]), ACT.Sigmoid)
+
+        g_codes, g_scales = quantise("g", interleave(nc.vector.tensor_copy, "g", g_raw[:], Q), Q)
+        gated(last, 0)
+        h_grouped0 = interleave(nc.vector.tensor_copy, "h0", hs_rows[0][:], HALF)
+        gated(last, 1)
+        h_q0 = quantise("h0", h_grouped0, HALF)
+        h_grouped1 = interleave(nc.vector.tensor_copy, "h1", hs_rows[1][:], HALF)
+        h_q1 = quantise("h1", h_grouped1, HALF)
+        c_ps = [ps.tile([P, HALF], F32, name="c_ps%d" % h) for h in range(2)]
+        for h, (h_codes, h_scales) in enumerate((h_q0, h_q1)):
+            nc.tensor.matmul_mx(out=c_ps[h][:], lhsT=g_codes[:].bitcast(FP8X4), lhsT_scale=g_scales[:],
+                                rhs=h_codes[:].bitcast(FP8X4), rhs_scale=h_scales[:], start=True, stop=True)
+
+        log_m = sbuf("log_m", [P, I], F32, tag="gate_pool%d" % last)
+        log_sum = sbuf("log_sum", [P, 1], F32)
+        nc.scalar.activation(log_m[:], dist[:], ACT.Ln, bias=0.5, accum_out=log_sum[:])
+        z_s = sbuf("z_s", [P, 1], F32)
+        p_s = sbuf("p_s", [P, I], F32)
+        inv_z = sbuf("inv_z", [P, 1], F32)
+        nc.vector.scalar_tensor_tensor(z_s[:], log_sum[:], -1.0 / GAIN, base[:], ALU.mult, ALU.add)
+        nc.vector.scalar_tensor_tensor(p_s[:], log_m[:], -1.0 / GAIN, relu_s[:], ALU.mult, ALU.add)
+        nc.vector.reciprocal(inv_z[:], z_s[:])
+        sig_z = sbuf("sig_z", [P, I], F32)
+        nc.scalar.activation(sig_z[:], sig[:], ACT.Copy, scale=inv_z[:])
+
+        shares = sbuf("shares", [P, I], F32)
+        mean = [sbuf("mean%d" % h, [P, 1], F32) for h in range(2)]
+        dp = sbuf("dp", [P, I], F32)
+        for h in range(2):
+            nc.vector.scalar_tensor_tensor(shares[:, halves[h]], c_ps[h][:], inv_z[:], p_s[:, halves[h]],
+                                           ALU.mult, ALU.mult, accum_out=mean[h][:])
+        for h in range(2):
+            nc.vector.tensor_scalar(dp[:, halves[h]], c_ps[h][:], mean[0][:], mean[1][:], ALU.subtract, ALU.subtract)
+        nc.vector.tensor_tensor(window[:].indirect(idx[:]), dp[:], sig_z[:], ALU.mult)
+
+        for c0 in range(0, T, STORE_COLS):
+            cols = slice(c0, c0 + STORE_COLS)
+            nc.vector.tensor_tensor(old_sb[:, cols], old_sb[:, cols], window[:, cols], ALU.add)
+            nc.sync.dma_start(out[:, cols], old_sb[:, cols])

@@ -70,8 +70,8 @@ def tile_attend_blrgated_capped_kernel(tc, query, keys_words, keys_scales, th, r
         load_scale_rows(key_bytes, keys_scales)
         nc.sync.dma_start(q_raw[:], query.rearrange("(p j) q -> p j q", j=PACK))
         nc.sync.dma_start(tab_wd[:].bitcast(I32), tab_words[0].bitcast(I32))
-        nc.sync.dma_start(idx2[:], offs2)
         nc.sync.dma_start(gate_pool[0][:], gtab_rows[0])
+        nc.sync.dma_start(idx2[:], offs2)
         load_scale_rows(tab_bytes, tab_scales)
         nc.sync.dma_start(w_raw[:], w1.rearrange("(p j) r -> p j r", j=PACK))
         for t in range(1, PACK):
@@ -81,12 +81,12 @@ def tile_attend_blrgated_capped_kernel(tc, query, keys_words, keys_scales, th, r
 
         nc.vector.memset(window[:], 0.0)
 
+        neg_half = sbuf("neg_half", [P, 1], F32)
+        nc.gpsimd.memset(neg_half[:], -0.5)
         neg_th = sbuf("neg_th", [P, 1], F32)
         neg_th_s = sbuf("neg_th_s", [P, 1], F32)
-        res_s = sbuf("res_s", [P, 1], F32)
         nc.gpsimd.tensor_scalar(neg_th[:], th_sb[:], -1.0, 0.0, ALU.mult, ALU.add)
         nc.gpsimd.tensor_scalar(neg_th_s[:], th_sb[:], -1.0 / GAIN, 0.0, ALU.mult, ALU.add)
-        nc.gpsimd.tensor_scalar(res_s[:], res_sb[:], 1.0 / GAIN, 0.0, ALU.mult, ALU.add)
 
         def quantise(name, grouped, cols):
             codes = sbuf(name + "_codes", [P, cols], U32)
@@ -94,8 +94,8 @@ def tile_attend_blrgated_capped_kernel(tc, query, keys_words, keys_scales, th, r
             nc.vector.quantize_mx(out=codes[:].bitcast(FP8X4), scales=scales[:], in_=grouped)
             return codes, scales
 
-        def interleave(copy, name, raw, cols):
-            grouped = sbuf(name + "_grouped", [P, cols, PACK], BF16)
+        def interleave(copy, name, raw, cols, tag=None):
+            grouped = sbuf(name + "_grouped", [P, cols, PACK], BF16, tag=tag)
             copy(grouped[:].rearrange("p (c i) t -> p c t i", i=4), raw.rearrange("p t (c i) -> p c t i", i=4))
             return grouped[:].rearrange("p c t -> p (c t)")
 
@@ -117,26 +117,30 @@ def tile_attend_blrgated_capped_kernel(tc, query, keys_words, keys_scales, th, r
         dist = sbuf("dist", [P, I], F32)
         nc.scalar.activation(sig[:], a_ps[:], ACT.Sigmoid, bias=neg_th[:])
         nc.scalar.activation(relu_s[:], a_ps[:], ACT.Relu, bias=neg_th_s[:], scale=1.0 / GAIN, accum_out=relu_sum[:])
-        nc.scalar.activation(dist[:], sig[:], ACT.Abs, bias=-0.5)
+        nc.scalar.activation(dist[:], sig[:], ACT.Abs, bias=neg_half[:])
         base = sbuf("base", [P, 1], F32)
-        nc.gpsimd.tensor_tensor(base[:], relu_sum[:], res_s[:], ALU.add)
+        nc.gpsimd.tensor_scalar(base[:], res_sb[:], 1.0 / GAIN, relu_sum[:], ALU.mult, ALU.add)
 
         t_words, t_bytes = gather_packed("tab", tab_wd, tab_bytes)
-        w_grouped = sbuf("w_grouped", [P, PACK, P, PACK], BF16)
-        nc.vector.tensor_copy(w_grouped[:].rearrange("p t m j -> p m j t"),
-                              w_raw[:].rearrange("p j (m t) -> p m j t", t=PACK))
-        w_codes, w_scales = quantise("w", w_grouped[:].rearrange("p t m j -> p (t m j)"), R)
+        w_dealt = w_raw[:].rearrange("p j (m t) -> p m j t", t=PACK)
+        w_q = []
+        for u in range(2):
+            w_grouped = sbuf("w_grouped%d" % u, [P, 2, P, PACK], BF16)
+            nc.vector.tensor_copy(w_grouped[:].rearrange("p t m j -> p m j t"), w_dealt[:, :, :, 2 * u: 2 * u + 2])
+            w_q.append(quantise("w%d" % u, w_grouped[:].rearrange("p t m j -> p (t m j)"), 2 * P))
         halves = [slice(h * HALF, (h + 1) * HALF) for h in range(2)]
         hs_rows = [sbuf("hs_rows%d" % h, [P, PACK, HALF], BF16) for h in range(2)]
         zh_ps = [ps.tile([P, I], F32, name="zh_ps%d" % t) for t in range(PACK)]
-        gate = [sbuf("gate%d" % t, [P, I], F32) for t in range(PACK)]
+        gate_tags = ("gate0", "neg_th_s", "neg_half", "gate3")
+        gate = [sbuf("gate%d" % t, [P, I], F32, tag=gate_tags[t]) for t in range(PACK)]
 
         def gated(t, h):
             nc.vector.scalar_tensor_tensor(hs_rows[h][:, t, :], zh_ps[t][:, halves[h]], hsc_sb[:, t: t + 1],
                                            gate[t][:, halves[h]], ALU.mult, ALU.mult)
 
         for t in range(PACK):
-            cols = slice(t * P, (t + 1) * P)
+            w_codes, w_scales = w_q[t // 2]
+            cols = slice(t % 2 * P, (t % 2 + 1) * P)
             nc.tensor.matmul_mx(out=zh_ps[t][:], lhsT=w_codes[:, cols].bitcast(FP8X4), lhsT_scale=w_scales[:, cols],
                                 rhs=t_words[:].bitcast(FP4X4), rhs_scale=t_bytes[:], start=True, stop=True)
         for t in range(PACK - 1):
@@ -148,7 +152,7 @@ def tile_attend_blrgated_capped_kernel(tc, query, keys_words, keys_scales, th, r
             nc.scalar.activation(gate[last][:, halves[h]],
                                  gate_pool[last][:].indirect(idx2[:, h * HALF // 16: (h + 1) * HALF // 16]), ACT.Sigmoid)
 
-        g_codes, g_scales = quantise("g", interleave(nc.vector.tensor_copy, "g", g_raw[:], Q), Q)
+        g_codes, g_scales = quantise("g", interleave(nc.vector.tensor_copy, "g", g_raw[:], Q, tag="neg_half"), Q)
         gated(last, 0)
         h_grouped0 = interleave(nc.vector.tensor_copy, "h0", hs_rows[0][:], HALF)
         gated(last, 1)
@@ -167,8 +171,11 @@ def tile_attend_blrgated_capped_kernel(tc, query, keys_words, keys_scales, th, r
         p_s = sbuf("p_s", [P, I], F32)
         inv_z = sbuf("inv_z", [P, 1], F32)
         nc.vector.scalar_tensor_tensor(z_s[:], log_sum[:], -1.0 / GAIN, base[:], ALU.mult, ALU.add)
-        nc.vector.scalar_tensor_tensor(p_s[:], log_m[:], -1.0 / GAIN, relu_s[:], ALU.mult, ALU.add)
-        nc.vector.reciprocal(inv_z[:], z_s[:])
+        for h in range(2):
+            nc.vector.scalar_tensor_tensor(p_s[:, halves[h]], log_m[:, halves[h]], -1.0 / GAIN, relu_s[:, halves[h]],
+                                           ALU.mult, ALU.add)
+            if h == 0:
+                nc.vector.reciprocal(inv_z[:], z_s[:])
         sig_z = sbuf("sig_z", [P, I], F32)
         nc.scalar.activation(sig_z[:], sig[:], ACT.Copy, scale=inv_z[:])
 

from contextlib import ExitStack

import concourse.mybir as mybir

D, K, R, T, I, Q, U = 512, 512, 512, 2048, 512, 128, 1024
FLOPS = 2 * D * Q * I + 2 * K * R * I + 2 * R * Q * I

F32 = mybir.dt.float32
BF16 = mybir.dt.bfloat16
I32 = mybir.dt.int32
U32 = mybir.dt.uint32
U16 = mybir.dt.uint16
U8 = mybir.dt.uint8
FP8X4 = mybir.dt.float8_e4m3fn_x4
FP4X4 = mybir.dt.float4_e2m1fn_x4
ACT = mybir.ActivationFunctionType
ALU = mybir.AluOpType

P = 128
PACK = 4
GAIN = 512.0
STORE_COLS = 512
HALF = I // 2


def tile_attend_blrgated_capped_kernel(tc, query, keys_words, keys_scales, th, reserve, tab_words, tab_scales,
                                        w1, gtab, gout, hsc, old, offs2, offs, out):
    nc = tc.nc
    with ExitStack() as ctx:
        sb = ctx.enter_context(tc.tile_pool(name="sb", bufs=1))
        ps = ctx.enter_context(tc.psum_pool(name="ps", bufs=1))

        def sbuf(name, shape, dtype, tag=None):
            return sb.tile(shape, dtype, name=name, tag=tag or name, align_bytes=64)

        idx = sbuf("idx", [P, I // 16], U16)
        idx2 = sbuf("idx2", [P, I // 16], U16)
        key_words = sbuf("key_words", [P, T], U16)
        key_bytes = sbuf("key_bytes", [P, T], U8)
        tab_wd = sbuf("tab_wd", [P, T], U16)
        tab_bytes = sbuf("tab_bytes", [P, T], U8)
        q_raw = sbuf("q_raw", [P, PACK, Q], F32)
        g_raw = sbuf("g_raw", [P, PACK, Q], F32)
        w_raw = sbuf("w_raw", [P, PACK, R], F32)
        gate_pool = [sbuf("gate_pool%d" % t, [P, U], F32) for t in range(PACK)]
        old_sb = sbuf("old_sb", [P, T], F32)
        th_sb = sbuf("th_sb", [P, 1], F32)
        res_sb = sbuf("res_sb", [P, 1], F32)
        hsc_sb = sbuf("hsc_sb", [P, PACK], F32)
        window = sbuf("window", [P, T], F32)
        warm = sbuf("warm", [P, 1], F32)
        warm_out = sbuf("warm_out", [P, 1], F32)

        nc.vector.memset(key_bytes[:].bitcast(I32), 0)
        nc.vector.memset(tab_bytes[:].bitcast(I32), 0)
        nc.gpsimd.memset(warm[:], 0.0)
        nc.scalar.activation(warm_out[:], warm[:], ACT.Sigmoid)

        def load_scale_rows(dst, src):
            for quad in range(4):
                nc.sync.dma_start(dst[32 * quad: 32 * quad + 4, :].bitcast(I32),
                                  src[0, 4 * quad: 4 * quad + 4, :].bitcast(I32))

        gtab_rows = gtab.rearrange("(p t) u -> t p u", t=PACK)
        nc.gpsimd.dma_start(th_sb[:], th)
        nc.gpsimd.dma_start(hsc_sb[:], hsc.rearrange("(p t) o -> p (t o)", t=PACK))
        nc.gpsimd.dma_start(res_sb[:], reserve)
        nc.sync.dma_start(idx[:], offs)
        nc.sync.dma_start(key_words[:].bitcast(I32), keys_words[0].bitcast(I32))
        load_scale_rows(key_bytes, keys_scales)
        nc.sync.dma_start(q_raw[:], query.rearrange("(p j) q -> p j q", j=PACK))
        nc.sync.dma_start(tab_wd[:].bitcast(I32), tab_words[0].bitcast(I32))
        nc.sync.dma_start(gate_pool[0][:], gtab_rows[0])
        nc.sync.dma_start(idx2[:], offs2)
        load_scale_rows(tab_bytes, tab_scales)
        nc.sync.dma_start(w_raw[:], w1.rearrange("(p j) r -> p j r", j=PACK))
        for t in range(1, PACK):
            nc.sync.dma_start(gate_pool[t][:], gtab_rows[t])
        nc.sync.dma_start(g_raw[:], gout.rearrange("(p j) q -> p j q", j=PACK))
        nc.sync.dma_start(old_sb[:], old)

        nc.vector.memset(window[:], 0.0)

        neg_half = sbuf("neg_half", [P, 1], F32)
        nc.gpsimd.memset(neg_half[:], -0.5)
        neg_th = sbuf("neg_th", [P, 1], F32)
        neg_th_s = sbuf("neg_th_s", [P, 1], F32)
        nc.gpsimd.tensor_scalar(neg_th[:], th_sb[:], -1.0, 0.0, ALU.mult, ALU.add)
        nc.gpsimd.tensor_scalar(neg_th_s[:], th_sb[:], -1.0 / GAIN, 0.0, ALU.mult, ALU.add)

        def quantise(name, grouped, cols):
            codes = sbuf(name + "_codes", [P, cols], U32)
            scales = sbuf(name + "_scales", [P, cols], U8)
            nc.vector.quantize_mx(out=codes[:].bitcast(FP8X4), scales=scales[:], in_=grouped)
            return codes, scales

        def interleave(copy, name, raw, cols, tag=None):
            grouped = sbuf(name + "_grouped", [P, cols, PACK], BF16, tag=tag)
            copy(grouped[:].rearrange("p (c i) t -> p c t i", i=4), raw.rearrange("p t (c i) -> p c t i", i=4))
            return grouped[:].rearrange("p c t -> p (c t)")

        def gather_packed(name, words, scale_bytes):
            got_words = sbuf(name + "_got_words", [P, I], U16)
            got_bytes = sbuf(name + "_got_bytes", [P, I], U8)
            nc.vector.tensor_copy(got_words[:], words[:].indirect(idx[:]))
            nc.vector.tensor_copy(got_bytes[:], scale_bytes[:].indirect(idx[:]))
            return got_words, got_bytes

        k_words, k_bytes = gather_packed("key", key_words, key_bytes)
        q_codes, q_scales = quantise("q", interleave(nc.scalar.copy, "q", q_raw[:], Q), Q)
        a_ps = ps.tile([P, I], F32, name="a_ps")
        nc.tensor.matmul_mx(out=a_ps[:], lhsT=q_codes[:].bitcast(FP8X4), lhsT_scale=q_scales[:],
                            rhs=k_words[:].bitcast(FP4X4), rhs_scale=k_bytes[:], start=True, stop=True)
        sig = sbuf("sig", [P, I], F32)
        relu_s = sbuf("relu_s", [P, I], F32)
        relu_sum = sbuf("relu_sum", [P, 1], F32)
        dist = sbuf("dist", [P, I], F32)
        nc.scalar.activation(sig[:], a_ps[:], ACT.Sigmoid, bias=neg_th[:])
        nc.scalar.activation(relu_s[:], a_ps[:], ACT.Relu, bias=neg_th_s[:], scale=1.0 / GAIN, accum_out=relu_sum[:])
        nc.scalar.activation(dist[:], sig[:], ACT.Abs, bias=neg_half[:])
        base = sbuf("base", [P, 1], F32)
        nc.gpsimd.tensor_scalar(base[:], res_sb[:], 1.0 / GAIN, relu_sum[:], ALU.mult, ALU.add)

        t_words, t_bytes = gather_packed("tab", tab_wd, tab_bytes)
        w_dealt = w_raw[:].rearrange("p j (m t) -> p m j t", t=PACK)
        w_q = []
        for u in range(2):
            w_grouped = sbuf("w_grouped%d" % u, [P, 2, P, PACK], BF16)
            nc.vector.tensor_copy(w_grouped[:].rearrange("p t m j -> p m j t"), w_dealt[:, :, :, 2 * u: 2 * u + 2])
            w_q.append(quantise("w%d" % u, w_grouped[:].rearrange("p t m j -> p (t m j)"), 2 * P))
        halves = [slice(h * HALF, (h + 1) * HALF) for h in range(2)]
        hs_rows = [sbuf("hs_rows%d" % h, [P, PACK, HALF], BF16) for h in range(2)]
        zh_ps = [ps.tile([P, I], F32, name="zh_ps%d" % t) for t in range(PACK)]
        gate_tags = ("gate0", "neg_th_s", "neg_half", "gate3")
        gate = [sbuf("gate%d" % t, [P, I], F32, tag=gate_tags[t]) for t in range(PACK)]

        def gated(t, h):
            nc.vector.scalar_tensor_tensor(hs_rows[h][:, t, :], zh_ps[t][:, halves[h]], hsc_sb[:, t: t + 1],
                                           gate[t][:, halves[h]], ALU.mult, ALU.mult)

        for t in range(PACK):
            w_codes, w_scales = w_q[t // 2]
            cols = slice(t % 2 * P, (t % 2 + 1) * P)
            nc.tensor.matmul_mx(out=zh_ps[t][:], lhsT=w_codes[:, cols].bitcast(FP8X4), lhsT_scale=w_scales[:, cols],
                                rhs=t_words[:].bitcast(FP4X4), rhs_scale=t_bytes[:], start=True, stop=True)
        for t in range(PACK - 1):
            nc.scalar.activation(gate[t][:], gate_pool[t][:].indirect(idx2[:]), ACT.Sigmoid)
            for h in range(2):
                gated(t, h)
        last = PACK - 1
        for h in range(2):
            nc.scalar.activation(gate[last][:, halves[h]],
                                 gate_pool[last][:].indirect(idx2[:, h * HALF // 16: (h + 1) * HALF // 16]), ACT.Sigmoid)

        g_codes, g_scales = quantise("g", interleave(nc.vector.tensor_copy, "g", g_raw[:], Q, tag="neg_half"), Q)
        gated(last, 0)
        h_grouped0 = interleave(nc.vector.tensor_copy, "h0", hs_rows[0][:], HALF)
        gated(last, 1)
        h_q0 = quantise("h0", h_grouped0, HALF)
        h_grouped1 = interleave(nc.vector.tensor_copy, "h1", hs_rows[1][:], HALF)
        h_q1 = quantise("h1", h_grouped1, HALF)
        c_ps = [ps.tile([P, HALF], F32, name="c_ps%d" % h) for h in range(2)]
        for h, (h_codes, h_scales) in enumerate((h_q0, h_q1)):
            nc.tensor.matmul_mx(out=c_ps[h][:], lhsT=g_codes[:].bitcast(FP8X4), lhsT_scale=g_scales[:],
                                rhs=h_codes[:].bitcast(FP8X4), rhs_scale=h_scales[:], start=True, stop=True)

        log_m = sbuf("log_m", [P, I], F32, tag="gate_pool%d" % last)
        log_sum = sbuf("log_sum", [P, 1], F32)
        nc.scalar.activation(log_m[:], dist[:], ACT.Ln, bias=0.5, accum_out=log_sum[:])
        z_s = sbuf("z_s", [P, 1], F32)
        p_s = sbuf("p_s", [P, I], F32)
        inv_z = sbuf("inv_z", [P, 1], F32)
        nc.vector.scalar_tensor_tensor(z_s[:], log_sum[:], -1.0 / GAIN, base[:], ALU.mult, ALU.add)
        for h in range(2):
            nc.vector.scalar_tensor_tensor(p_s[:, halves[h]], log_m[:, halves[h]], -1.0 / GAIN, relu_s[:, halves[h]],
                                           ALU.mult, ALU.add)
            if h == 0:
                nc.vector.reciprocal(inv_z[:], z_s[:])
        sig_z = sbuf("sig_z", [P, I], F32)
        nc.scalar.activation(sig_z[:], sig[:], ACT.Copy, scale=inv_z[:])

        shares = sbuf("shares", [P, I], F32)
        mean = [sbuf("mean%d" % h, [P, 1], F32) for h in range(2)]
        dp = sbuf("dp", [P, I], F32)
        for h in range(2):
            nc.vector.scalar_tensor_tensor(shares[:, halves[h]], c_ps[h][:], inv_z[:], p_s[:, halves[h]],
                                           ALU.mult, ALU.mult, accum_out=mean[h][:])
        for h in range(2):
            nc.vector.tensor_scalar(dp[:, halves[h]], c_ps[h][:], mean[0][:], mean[1][:], ALU.subtract, ALU.subtract)
        nc.vector.tensor_tensor(window[:].indirect(idx[:]), dp[:], sig_z[:], ALU.mult)

        for c0 in range(0, T, STORE_COLS):
            cols = slice(c0, c0 + STORE_COLS)
            nc.vector.tensor_tensor(old_sb[:, cols], old_sb[:, cols], window[:, cols], ALU.add)
            nc.sync.dma_start(out[:, cols], old_sb[:, cols])
